import numpy as np
import ml_dtypes


def mxq(x, axis, fmt="e4m3"):
    dtype, down = {"e4m3": (ml_dtypes.float8_e4m3fn, 7), "e5m2": (ml_dtypes.float8_e5m2, 14)}[fmt]
    v = np.moveaxis(np.asarray(x, np.float32).astype(ml_dtypes.bfloat16).astype(np.float64), axis, -1)
    blocks = v.reshape(v.shape[:-1] + (-1, 32))
    amax = np.abs(blocks).max(-1, keepdims=True)
    byte = np.maximum(np.where(amax > 0, np.frexp(amax)[1] - 1 + 127, 0) - down, 1)
    scale = np.exp2(byte - 127.0)
    codes = (blocks / scale).astype(np.float32).astype(dtype).astype(np.float64)
    return np.moveaxis((codes * scale).reshape(v.shape), -1, axis)


WIDE = False


def mx_kscale(k):
    if not WIDE:
        return np.ones(k)
    levels = np.array([10, -10, 5, -5, 0])
    if k % 512:
        return np.exp2(np.random.permutation(np.resize(levels, k // 32))).repeat(32)
    a = np.empty((k // 512, 16))
    for p in range(k // 512):
        a[p, :8] = np.random.permutation(np.resize(levels, 8))
        for g in range(8):
            far = levels[np.abs(levels - a[p, g]) >= 10]
            a[p, g + 8] = far[np.random.randint(len(far))]
    return np.exp2(a.ravel()).repeat(32)


BF16 = ml_dtypes.bfloat16


def bf(x):
    return np.asarray(x, np.float32).astype(BF16)


def f64(x):
    return np.asarray(x).astype(np.float64)


E2M1 = np.array([0.0, 0.5, 1.0, 1.5, 2.0, 3.0, 4.0, 6.0, -0.0, -0.5, -1.0, -1.5, -2.0, -3.0, -4.0, -6.0])


def pack_weight(w, fmt):
    k, n = w.shape
    w = f64(bf(w)).reshape(k // 32, 32, n)
    amax = np.abs(w).max(1)
    if fmt == "e4m3":
        byte = np.frexp(amax)[1] - 1 + 127 - 7
    else:
        mant, ex = np.frexp(amax / 6.0)
        byte = np.where(mant > 0.5, ex, ex - 1) + 127
    byte = np.clip(np.where(amax > 0, byte, 1), 1, 254)
    scaled = (w * np.exp2(127.0 - byte)[:, None, :]).reshape(k, n).astype(np.float32)
    by_word = np.ascontiguousarray(scaled.reshape(k // 512, 128, 4, n).transpose(0, 1, 3, 2))
    if fmt == "e4m3":
        words = by_word.astype(ml_dtypes.float8_e4m3fn).view(np.uint8)
    else:
        c = by_word.astype(ml_dtypes.float4_e2m1fn).view(np.uint8) & 0xF
        words = c[..., 0::2] | (c[..., 1::2] << 4)
    return np.ascontiguousarray(words), np.ascontiguousarray(byte.astype(np.uint8).reshape(k // 512, 16, n))


def unpack_weight(words, scales, fmt):
    g, p, n, _ = words.shape
    if fmt == "e4m3":
        vals = np.ascontiguousarray(words).view(ml_dtypes.float8_e4m3fn).astype(np.float64)
    else:
        nib = np.empty((g, p, n, 4), np.uint8)
        nib[..., 0::2] = words & 0xF
        nib[..., 1::2] = words >> 4
        vals = E2M1[nib]
    vals = vals * np.repeat(np.exp2(scales.astype(np.float64) - 127.0), 8, axis=1)[..., None]
    return vals.transpose(0, 1, 3, 2).reshape(g * 512, n)
def pack4(w):
    words, scales = pack_weight(w, "e2m1")
    return words.reshape(words.shape[0], 128, -1), scales


def unpack4(words, scales):
    return unpack_weight(words.reshape(words.shape[0], 128, -1, 2), scales, "e2m1")


S, P, C, R = 2048, 512, 1024, 512


def setup_inputs():
    s = mx_kscale(S)
    u = mx_kscale(C)
    t = mx_kscale(S)
    v = np.square(np.random.standard_normal((S, S))) / np.sqrt(3 * S)
    y = np.random.standard_normal((S, P))
    v_words, v_scales = pack4(v * s[:, None])
    y_words, y_scales = pack4(y / s[:, None])
    return {"v_words": v_words, "v_scales": v_scales,
            "y_words": y_words, "y_scales": y_scales,
            "x": bf(np.random.standard_normal((S, P)) * t[:, None]),
            "cov": bf(np.random.standard_normal((S, C)) * u / t[:, None]),
            "load": bf(np.random.standard_normal((C, R)) / np.sqrt(C) / u[:, None])}


def reference(v_words, v_scales, y_words, y_scales, x, cov, load):
    lag = unpack4(v_words, v_scales).T @ unpack4(y_words, y_scales)
    local = f64(x) * lag
    score = mxq(f64(cov), 1, "e4m3") @ mxq(f64(load), 0, "e4m3")
    member = np.maximum(score, 0.0)
    assoc = mxq(local, 0, "e4m3").T @ mxq(member, 0, "e4m3")
    return assoc / np.sqrt(S)

@@ -1,0 +1,410 @@
+import math
+from contextlib import ExitStack
+
+import concourse.mybir as mybir
+from concourse.masks import make_identity
+
+S, PAIRS, C, R = 2048, 512, 1024, 512
+FLOPS = 2 * S * S * PAIRS + 2 * S * C * R + 2 * S * PAIRS * R
+
+F32 = mybir.dt.float32
+BF16 = mybir.dt.bfloat16
+I32 = mybir.dt.int32
+U32 = mybir.dt.uint32
+U8 = mybir.dt.uint8
+FP8X4 = mybir.dt.float8_e4m3fn_x4
+FP4X4 = mybir.dt.float4_e2m1fn_x4
+ACT = mybir.ActivationFunctionType
+ALU = mybir.AluOpType
+
+P = 128
+K_PASS = 512
+GROUPS = S // K_PASS
+LAG_PASSES = S // K_PASS
+COV_PASSES = C // K_PASS
+HALF = 256
+BANKS = 8
+
+
+def tile_local_moran_typology_s12_kernel(tc, v_words, v_scales, y_words, y_scales, x, cov, load, out):
+    nc = tc.nc
+    with ExitStack() as ctx:
+        keep = ctx.enter_context(tc.tile_pool(name="keep", bufs=1))
+        work = ctx.enter_context(tc.tile_pool(name="work", bufs=2))
+        psum = ctx.enter_context(tc.psum_pool(name="psum", bufs=1))
+        ctx.enter_context(tc.manual_schedule())
+
+        tiles = {}
+        ring = list(range(BANKS))
+
+        def kept(key, shape, dtype):
+            name = "t_" + "_".join(str(part) for part in key)
+            tiles[key] = keep.tile(shape, dtype, name=name, align_bytes=64)
+            return tiles[key]
+
+        def passing(key, shape, dtype, bufs):
+            name = "t_" + "_".join(str(part) for part in key)
+            tiles[key] = work.tile(shape, dtype, name=name, tag=key[0], bufs=bufs, align_bytes=64)
+            return tiles[key]
+
+        def bank(key):
+            number = ring.pop(0)
+            ring.append(number)
+            name = "b_" + "_".join(str(part) for part in key)
+            tiles[key] = psum.tile([P, 512], F32, name=name, tag="bank%d" % number)
+            return tiles[key]
+
+        def load_scale_rows(plane, scales, cols, rows):
+            by_row = scales.rearrange("g (q r) n -> r q g n", r=4)
+            for r in rows:
+                nc.sync.dma_start(out=plane[r:P:32, :, :], in_=by_row[r][:, :, cols].bitcast(I32))
+
+        def load_v(g, passes):
+            raw = passing(("v_raw", g, passes[0]), [P, len(passes), 256], I32, 4)
+            words = v_words[passes[0] : passes[-1] + 1, :, 1024 * g : 1024 * (g + 1)]
+            nc.sync.dma_start(out=raw[:], in_=words.rearrange("c p n -> p c n").bitcast(I32))
+
+        def load_y(passes):
+            codes = kept(("y", passes[0]), [P, len(passes) * 1024], U8)
+            words = y_words[passes[0] : passes[-1] + 1, :, :]
+            nc.sync.dma_start(
+                out=codes[:].bitcast(I32).rearrange("p (c n) -> p c n", c=len(passes)),
+                in_=words.rearrange("c p n -> p c n").bitcast(I32),
+            )
+            for i, c in enumerate(passes):
+                tiles["y_pass", c] = codes[:, 1024 * i : 1024 * (i + 1)]
+
+        def load_x(g):
+            rows = passing(("x", g), [P, 4, PAIRS], BF16, 4)
+            by_lane = x[K_PASS * g : K_PASS * (g + 1), :].rearrange("(a t l) n -> l a t n", t=4, l=4)
+            for lane in range(4):
+                nc.sync.dma_start(out=rows[lane:P:4, :, :], in_=by_lane[lane])
+
+        def load_cov(g, b):
+            raw = passing(("cov_raw", g, b), [P, 2 * C], BF16, 4)
+            first = K_PASS * g + 256 * b
+            nc.sync.dma_start(
+                out=raw[:].rearrange("p (a k) -> p a k", a=2),
+                in_=cov[first : first + 256, :].rearrange("(a p) k -> p a k", p=P),
+            )
+
+        def load_loadings(c):
+            raw = kept(("load_raw", c), [P, 4, R], BF16)
+            nc.sync.dma_start(out=raw[:], in_=load[K_PASS * c : K_PASS * (c + 1), :].rearrange("(p j) n -> p j n", j=4))
+
+        def sort_v(g, passes):
+            n = len(passes)
+            codes = passing(("v", g, passes[0]), [P, n * 1024], U8, 4)
+            nc.vector.tensor_copy(
+                out=codes[:].bitcast(I32).rearrange("p (c t a l) -> p c t a l", c=n, t=4, l=2),
+                in_=tiles["v_raw", g, passes[0]][:].rearrange("p c (a t l) -> p c t a l", t=4, l=2),
+            )
+            for i, c in enumerate(passes):
+                tiles["v_pass", g, c] = codes[:, 1024 * i : 1024 * (i + 1)]
+
+        def sort_v_scales(g):
+            plane = passing(("v_scale", g), [P, LAG_PASSES * 512], U8, 2)
+            nc.vector.tensor_copy(
+                out=plane[:].bitcast(I32).rearrange("p (c t a b) -> p c a t b", c=LAG_PASSES, t=4, b=4),
+                in_=v_scale_raw[g][:].rearrange("p c (a b t) -> p c a t b", b=4, t=4),
+            )
+
+        def interleave_loadings(c, cols, copy):
+            if ("load_in", c) not in tiles:
+                kept(("load_in", c), [P, 4 * R], BF16)
+            grouped = tiles["load_in", c][:, 4 * cols.start : 4 * cols.stop]
+            copy(
+                out=grouped.rearrange("p (n i j) -> p n j i", i=4, j=4),
+                in_=tiles["load_raw", c][:, :, cols].rearrange("p j (n i) -> p n j i", i=4),
+            )
+
+        def quantize(name, index, cols, source):
+            if (name, index) not in tiles:
+                kept((name, index), [P, 512], U32)
+                kept((name + "_scale", index), [P, 512], U8)
+            nc.vector.quantize_mx(
+                out=tiles[name, index][:, cols].bitcast(FP8X4),
+                scales=tiles[name + "_scale", index][:, cols],
+                in_=source[:],
+            )
+
+        def quantize_loadings(c):
+            quantize("load", c, slice(0, 512), tiles["load_in", c])
+
+        def sort_cov(g, b, copy):
+            words = passing(("cov_words", g, b), [P, C], F32, 4)
+            copy(
+                out=words[:].rearrange("p (j u k) -> p j u k", u=2, k=P),
+                in_=tiles["cov_raw", g, b][:].bitcast(F32).rearrange("p (j k u) -> p j u k", u=2, k=P),
+            )
+
+        def transpose_cov(g):
+            for b in range(2):
+                for c in range(COV_PASSES):
+                    turned = bank(("cov_t", g, c, b))
+                    words = tiles["cov_words", g, b]
+                    for u in range(2):
+                        for a in range(2):
+                            src = (2 * (COV_PASSES * a + c) + u) * P
+                            dst = (2 * u + a) * P
+                            nc.tensor.transpose(turned[:, dst : dst + P], words[:, src : src + P], identity[:])
+
+        def drain_cov(g, c, b):
+            if b == 0:
+                passing(("cov_in", g, c), [P, 2048], BF16, 3)
+            dst = tiles["cov_in", g, c][:].bitcast(F32).rearrange("p (t w) -> p t w", t=4)[:, :, P * b : P * (b + 1)]
+            nc.scalar.copy(
+                out=dst.rearrange("p t (a l u) -> p t a l u", l=4, u=2),
+                in_=tiles["cov_t", g, c, b][:].rearrange("p (u a t l) -> p t a l u", u=2, t=4, l=4),
+            )
+
+        def quantize_cov(g, c):
+            quantize("cov", COV_PASSES * g + c, slice(0, 512), tiles["cov_in", g, c])
+
+        def lag_pass(g, h, u, e, c):
+            t = 2 * u + e
+            nc.tensor.matmul_mx(
+                out=tiles["lag", g, h, u][:, HALF * e : HALF * (e + 1)],
+                lhsT=tiles["v_pass", g, c][:, 256 * t : 256 * (t + 1)].bitcast(FP4X4),
+                lhsT_scale=tiles["v_scale", g][:, 512 * c + P * t : 512 * c + P * (t + 1)],
+                rhs=tiles["y_pass", c][:, 2 * HALF * h : 2 * HALF * (h + 1)].bitcast(FP4X4),
+                rhs_scale=y_scale[:, 512 * c + HALF * h : 512 * c + HALF * (h + 1)],
+                start=(c == 0),
+                stop=(c == LAG_PASSES - 1),
+            )
+
+        def score_pass(g, h, u, e, c):
+            t = 2 * u + e
+            index = COV_PASSES * g + c
+            nc.tensor.matmul_mx(
+                out=tiles["score", g, h, u][:, HALF * e : HALF * (e + 1)],
+                lhsT=tiles["cov", index][:, P * t : P * (t + 1)].bitcast(FP8X4),
+                lhsT_scale=tiles["cov_scale", index][:, P * t : P * (t + 1)],
+                rhs=tiles["load", c][:, HALF * h : HALF * (h + 1)].bitcast(FP8X4),
+                rhs_scale=tiles["load_scale", c][:, HALF * h : HALF * (h + 1)],
+                start=(c == 0),
+                stop=(c == COV_PASSES - 1),
+            )
+
+        def first_stage(name, one_pass, passes, g, halves):
+            banks = [(h, u) for h in halves for u in range(2)]
+            for h, u in banks:
+                bank((name, g, h, u))
+            for c in range(passes):
+                for h, u in banks:
+                    one_pass(g, h, u, 0, c)
+            for h, u in banks:
+                for c in range(passes):
+                    one_pass(g, h, u, 1, c)
+
+        def lag(g, halves):
+            first_stage("lag", lag_pass, LAG_PASSES, g, halves)
+
+        def score(g, halves):
+            first_stage("score", score_pass, COV_PASSES, g, halves)
+
+        def pair_view(name, g, h, u):
+            if u == 0:
+                passing((name + "_pairs", g, h), [P, 4 * HALF], BF16, 6)
+            pairs = tiles[name + "_pairs", g, h][:, 2 * HALF * u : 2 * HALF * (u + 1)]
+            return pairs.rearrange("p (n e) -> p n e", e=2)
+
+        def local(g, h, u):
+            nc.vector.tensor_tensor(
+                out=pair_view("local", g, h, u),
+                in0=tiles["lag", g, h, u][:].rearrange("p (e n) -> p n e", e=2),
+                in1=tiles["x", g][:, 2 * u : 2 * u + 2, HALF * h : HALF * (h + 1)].rearrange("p e n -> p n e"),
+                op=ALU.mult,
+            )
+
+        def member(g, h, u):
+            nc.scalar.activation(
+                out=pair_view("member", g, h, u),
+                in_=tiles["score", g, h, u][:].rearrange("p (e n) -> p n e", e=2),
+                func=ACT.Relu,
+            )
+
+        def join_pairs(name, g, h):
+            grouped = passing((name + "_in", g, h), [P, 4 * HALF], BF16, 2)
+            nc.vector.tensor_copy(
+                out=grouped[:].bitcast(F32).rearrange("p (n u) -> p n u", u=2),
+                in_=tiles[name + "_pairs", g, h][:].bitcast(F32).rearrange("p (u n) -> p n u", u=2),
+            )
+
+        def quantize_half(name, g, h):
+            quantize(name, g, slice(HALF * h, HALF * (h + 1)), tiles[name + "_in", g, h])
+
+        def finish(name, g):
+            join_pairs(name, g, 0)
+            join_pairs(name, g, 1)
+            quantize_half(name, g, 0)
+            quantize_half(name, g, 1)
+
+        def drain_group(g):
+            for c in range(COV_PASSES):
+                for b in range(2):
+                    drain_cov(g, c, b)
+
+        def score_group(g):
+            for h in range(2):
+                score(g, [h])
+                member(g, h, 0)
+                member(g, h, 1)
+
+        def load_v_scales(g):
+            load_scale_rows(v_scale_raw[g], v_scales, slice(512 * g, 512 * (g + 1)), range(4))
+
+        def assoc(m, cols, scale_out):
+            width = cols.stop - cols.start
+            sums = bank(("assoc", m, cols.start))
+            for g in range(GROUPS):
+                nc.tensor.matmul_mx(
+                    out=sums[:, 0:width],
+                    lhsT=tiles["local", g][:, P * m : P * (m + 1)].bitcast(FP8X4),
+                    lhsT_scale=tiles["local_scale", g][:, P * m : P * (m + 1)],
+                    rhs=tiles["member", g][:, cols].bitcast(FP8X4),
+                    rhs_scale=tiles["member_scale", g][:, cols],
+                    start=(g == 0),
+                    stop=(g == GROUPS - 1),
+                )
+            result = kept(("out", m, cols.start), [P, width], F32)
+            scale_out(result[:], sums[:, 0:width])
+            nc.sync.dma_start(out=out[P * m : P * (m + 1), cols], in_=result[:])
+
+        def scale_on_scalar(result, sums):
+            nc.scalar.activation(out=result, in_=sums, func=ACT.Copy, scale=1.0 / math.sqrt(S))
+
+        def scale_on_vector(result, sums):
+            nc.vector.tensor_scalar_mul(out=result, in0=sums, scalar1=1.0 / math.sqrt(S))
+
+        v_scale_raw = [kept(("v_scale_raw", g), [P, LAG_PASSES, P], I32) for g in range(GROUPS)]
+        y_scale = kept(("y_scale",), [P, LAG_PASSES * 512], U8)
+        y_scale_words = y_scale[:].bitcast(I32).rearrange("p (c n) -> p c n", c=LAG_PASSES)
+        identity = kept(("identity",), [P, P], F32)
+        warm = kept(("warm",), [P, 2], F32)
+        nc.vector.memset(v_scale_raw[0][:], 0)
+        nc.vector.memset(y_scale_words, 0)
+        for g in range(1, GROUPS):
+            nc.vector.memset(v_scale_raw[g][:], 0)
+        nc.vector.memset(identity[:], 0.0)
+        make_identity(nc, identity[:], nomemset=True)
+        nc.scalar.activation(out=warm[:, 0:1], in_=identity[:, 0:1], func=ACT.Relu)
+
+        pieces = [[0], [1], [2, 3]]
+        whole = [0, 1, 2, 3]
+        load_v_scales(0)
+        load_scale_rows(y_scale_words, y_scales, slice(0, 512), range(2))
+        load_v(0, pieces[0])
+        load_y(pieces[0])
+        load_scale_rows(y_scale_words, y_scales, slice(0, 512), range(2, 4))
+        for piece in pieces[1:]:
+            load_v(0, piece)
+            load_y(piece)
+        load_v_scales(1)
+        load_v(1, whole)
+        load_loadings(0)
+        load_x(0)
+        load_cov(0, 0)
+        load_cov(0, 1)
+        load_x(1)
+
+        sort_v_scales(0)
+        for piece in pieces:
+            sort_v(0, piece)
+        load_v_scales(2)
+        load_v(2, whole)
+        load_cov(1, 0)
+        load_loadings(1)
+        load_cov(1, 1)
+        load_x(2)
+        lag(0, [0, 1])
+        sort_v_scales(1)
+        sort_v(1, whole)
+        interleave_loadings(0, slice(0, R), nc.vector.tensor_copy)
+        lag(1, [0])
+        lag(1, [1])
+        local(0, 0, 0)
+        quantize_loadings(0)
+        local(0, 0, 1)
+        local(0, 1, 0)
+        local(0, 1, 1)
+        sort_cov(0, 0, nc.scalar.copy)
+        sort_cov(0, 1, nc.scalar.copy)
+        load_cov(2, 0)
+        load_cov(2, 1)
+        load_v_scales(3)
+        load_v(3, whole)
+        join_pairs("local", 0, 0)
+        local(1, 0, 0)
+        quantize_half("local", 0, 0)
+        local(1, 0, 1)
+        sort_v_scales(2)
+        sort_v(2, whole)
+        local(1, 1, 0)
+        local(1, 1, 1)
+        transpose_cov(0)
+        lag(2, [0])
+        drain_group(0)
+        sort_cov(1, 0, nc.vector.tensor_copy)
+        quantize_cov(0, 0)
+        interleave_loadings(1, slice(0, HALF), nc.vector.tensor_copy)
+        interleave_loadings(1, slice(HALF, R), nc.scalar.copy)
+        sort_cov(1, 1, nc.vector.tensor_copy)
+        quantize_cov(0, 1)
+        load_cov(3, 0)
+        load_cov(3, 1)
+        load_x(3)
+        quantize_loadings(1)
+        local(2, 0, 0)
+        local(2, 0, 1)
+
+        transpose_cov(1)
+        drain_group(1)
+        score_group(0)
+        lag(2, [1])
+        join_pairs("local", 0, 1)
+        quantize_cov(1, 0)
+        sort_cov(2, 0, nc.vector.tensor_copy)
+        quantize_cov(1, 1)
+        sort_cov(2, 1, nc.vector.tensor_copy)
+        quantize_half("local", 0, 1)
+        local(2, 1, 0)
+        local(2, 1, 1)
+
+        transpose_cov(2)
+        drain_group(2)
+        score_group(1)
+        sort_v_scales(3)
+        sort_v(3, whole)
+        lag(3, [0])
+        finish("member", 0)
+        quantize_cov(2, 0)
+        sort_cov(3, 0, nc.vector.tensor_copy)
+        quantize_cov(2, 1)
+        sort_cov(3, 1, nc.vector.tensor_copy)
+        finish("local", 1)
+        local(3, 0, 0)
+        local(3, 0, 1)
+
+        transpose_cov(3)
+        drain_group(3)
+        score_group(2)
+        finish("member", 1)
+        quantize_cov(3, 0)
+        join_pairs("local", 3, 0)
+        quantize_cov(3, 1)
+        quantize_half("local", 3, 0)
+        finish("local", 2)
+
+        score_group(3)
+        lag(3, [1])
+        finish("member", 2)
+        finish("member", 3)
+        local(3, 1, 0)
+        local(3, 1, 1)
+        join_pairs("local", 3, 1)
+        quantize_half("local", 3, 1)
+        for m in range(3):
+            assoc(m, slice(0, R), scale_on_scalar)
+        assoc(3, slice(0, HALF), scale_on_scalar)
+        assoc(3, slice(HALF, R), scale_on_vector)

@@ -36,6 +36,7 @@ def tile_local_moran_typology_s12_kernel(tc, v_words, v_scales, y_words, y_scale
 
         tiles = {}
         ring = list(range(BANKS))
+        held = {}
 
         def kept(key, shape, dtype):
             name = "t_" + "_".join(str(part) for part in key)
@@ -49,10 +50,13 @@ def tile_local_moran_typology_s12_kernel(tc, v_words, v_scales, y_words, y_scale
 
         def bank(key):
             number = ring.pop(0)
-            ring.append(number)
+            held[key] = number
             name = "b_" + "_".join(str(part) for part in key)
             tiles[key] = psum.tile([P, 512], F32, name=name, tag="bank%d" % number)
             return tiles[key]
+
+        def release(key):
+            ring.append(held[key])
 
         def load_scale_rows(plane, scales, cols, rows):
             by_row = scales.rearrange("g (q r) n -> r q g n", r=4)
@@ -125,11 +129,11 @@ def tile_local_moran_typology_s12_kernel(tc, v_words, v_scales, y_words, y_scale
             nc.vector.quantize_mx(
                 out=tiles[name, index][:, cols].bitcast(FP8X4),
                 scales=tiles[name + "_scale", index][:, cols],
-                in_=source[:],
+                in_=source,
             )
 
-        def quantize_loadings(c):
-            quantize("load", c, slice(0, 512), tiles["load_in", c])
+        def quantize_loadings(c, cols):
+            quantize("load", c, cols, tiles["load_in", c][:, 4 * cols.start : 4 * cols.stop])
 
         def sort_cov(g, b, copy):
             words = passing(("cov_words", g, b), [P, C], F32, 4)
@@ -139,8 +143,8 @@ def tile_local_moran_typology_s12_kernel(tc, v_words, v_scales, y_words, y_scale
             )
 
         def transpose_cov(g):
-            for b in range(2):
-                for c in range(COV_PASSES):
+            for c in range(COV_PASSES):
+                for b in range(2):
                     turned = bank(("cov_t", g, c, b))
                     words = tiles["cov_words", g, b]
                     for u in range(2):
@@ -149,17 +153,18 @@ def tile_local_moran_typology_s12_kernel(tc, v_words, v_scales, y_words, y_scale
                             dst = (2 * u + a) * P
                             nc.tensor.transpose(turned[:, dst : dst + P], words[:, src : src + P], identity[:])
 
-        def drain_cov(g, c, b):
+        def drain_cov(g, c, b, copy):
             if b == 0:
                 passing(("cov_in", g, c), [P, 2048], BF16, 3)
             dst = tiles["cov_in", g, c][:].bitcast(F32).rearrange("p (t w) -> p t w", t=4)[:, :, P * b : P * (b + 1)]
-            nc.scalar.copy(
+            copy(
                 out=dst.rearrange("p t (a l u) -> p t a l u", l=4, u=2),
                 in_=tiles["cov_t", g, c, b][:].rearrange("p (u a t l) -> p t a l u", u=2, t=4, l=4),
             )
+            release(("cov_t", g, c, b))
 
         def quantize_cov(g, c):
-            quantize("cov", COV_PASSES * g + c, slice(0, 512), tiles["cov_in", g, c])
+            quantize("cov", COV_PASSES * g + c, slice(0, 512), tiles["cov_in", g, c][:])
 
         def lag_pass(g, h, u, e, c):
             t = 2 * u + e
@@ -173,83 +178,87 @@ def tile_local_moran_typology_s12_kernel(tc, v_words, v_scales, y_words, y_scale
                 stop=(c == LAG_PASSES - 1),
             )
 
-        def score_pass(g, h, u, e, c):
-            t = 2 * u + e
-            index = COV_PASSES * g + c
-            nc.tensor.matmul_mx(
-                out=tiles["score", g, h, u][:, HALF * e : HALF * (e + 1)],
-                lhsT=tiles["cov", index][:, P * t : P * (t + 1)].bitcast(FP8X4),
-                lhsT_scale=tiles["cov_scale", index][:, P * t : P * (t + 1)],
-                rhs=tiles["load", c][:, HALF * h : HALF * (h + 1)].bitcast(FP8X4),
-                rhs_scale=tiles["load_scale", c][:, HALF * h : HALF * (h + 1)],
-                start=(c == 0),
-                stop=(c == COV_PASSES - 1),
-            )
-
-        def first_stage(name, one_pass, passes, g, halves):
-            banks = [(h, u) for h in halves for u in range(2)]
-            for h, u in banks:
-                bank((name, g, h, u))
-            for c in range(passes):
-                for h, u in banks:
-                    one_pass(g, h, u, 0, c)
-            for h, u in banks:
-                for c in range(passes):
-                    one_pass(g, h, u, 1, c)
+        def lag_half(g, h):
+            for u in range(2):
+                bank(("lag", g, h, u))
+                for e in range(2):
+                    for c in range(LAG_PASSES):
+                        lag_pass(g, h, u, e, c)
 
         def lag(g, halves):
-            first_stage("lag", lag_pass, LAG_PASSES, g, halves)
+            banks = [(h, u) for h in halves for u in range(2)]
+            for h, u in banks:
+                bank(("lag", g, h, u))
+            for c in range(LAG_PASSES):
+                for h, u in banks:
+                    lag_pass(g, h, u, 0, c)
+            for h, u in banks:
+                for c in range(LAG_PASSES):
+                    lag_pass(g, h, u, 1, c)
 
-        def score(g, halves):
-            first_stage("score", score_pass, COV_PASSES, g, halves)
+        def score(g, q):
+            sums = bank(("score", g, q))
+            for t in range(4):
+                for c in range(COV_PASSES):
+                    index = COV_PASSES * g + c
+                    nc.tensor.matmul_mx(
+                        out=sums[:, P * t : P * (t + 1)],
+                        lhsT=tiles["cov", index][:, P * t : P * (t + 1)].bitcast(FP8X4),
+                        lhsT_scale=tiles["cov_scale", index][:, P * t : P * (t + 1)],
+                        rhs=tiles["load", c][:, P * q : P * (q + 1)].bitcast(FP8X4),
+                        rhs_scale=tiles["load_scale", c][:, P * q : P * (q + 1)],
+                        start=(c == 0),
+                        stop=(c == COV_PASSES - 1),
+                    )
 
         def pair_view(name, g, h, u):
-            if u == 0:
-                passing((name + "_pairs", g, h), [P, 4 * HALF], BF16, 6)
-            pairs = tiles[name + "_pairs", g, h][:, 2 * HALF * u : 2 * HALF * (u + 1)]
-            return pairs.rearrange("p (n e) -> p n e", e=2)
+            if (name + "_pairs", g) not in tiles:
+                passing((name + "_pairs", g), [P, 4 * 512], BF16, 3)
+            first = 2 * HALF * (2 * h + u)
+            pairs = tiles[name + "_pairs", g][:, first : first + 2 * HALF]
+            return pairs.rearrange("p (n i e) -> p n e i", i=4, e=2)
 
         def local(g, h, u):
             nc.vector.tensor_tensor(
                 out=pair_view("local", g, h, u),
-                in0=tiles["lag", g, h, u][:].rearrange("p (e n) -> p n e", e=2),
-                in1=tiles["x", g][:, 2 * u : 2 * u + 2, HALF * h : HALF * (h + 1)].rearrange("p e n -> p n e"),
+                in0=tiles["lag", g, h, u][:].rearrange("p (e n i) -> p n e i", e=2, i=4),
+                in1=tiles["x", g][:, 2 * u : 2 * u + 2, HALF * h : HALF * (h + 1)].rearrange("p e (n i) -> p n e i", i=4),
                 op=ALU.mult,
             )
+            release(("lag", g, h, u))
 
-        def member(g, h, u):
+        def member(g, q):
+            if q == 0:
+                passing(("member_in", g), [P, 4 * 512], BF16, 2)
             nc.scalar.activation(
-                out=pair_view("member", g, h, u),
-                in_=tiles["score", g, h, u][:].rearrange("p (e n) -> p n e", e=2),
+                out=tiles["member_in", g][:, 4 * P * q : 4 * P * (q + 1)].rearrange("p (n t) -> p n t", t=4),
+                in_=tiles["score", g, q][:].rearrange("p (t n) -> p n t", t=4),
                 func=ACT.Relu,
             )
+            release(("score", g, q))
 
-        def join_pairs(name, g, h):
-            grouped = passing((name + "_in", g, h), [P, 4 * HALF], BF16, 2)
+        def join_pairs(name, g, halves):
+            if (name + "_in", g) not in tiles:
+                passing((name + "_in", g), [P, 4 * 512], BF16, 2)
+            words = slice(2 * HALF * halves[0], 2 * HALF * (halves[-1] + 1))
             nc.vector.tensor_copy(
-                out=grouped[:].bitcast(F32).rearrange("p (n u) -> p n u", u=2),
-                in_=tiles[name + "_pairs", g, h][:].bitcast(F32).rearrange("p (u n) -> p n u", u=2),
+                out=tiles[name + "_in", g][:].bitcast(F32)[:, words].rearrange("p (h n u) -> p h n u", n=HALF, u=2),
+                in_=tiles[name + "_pairs", g][:].bitcast(F32)[:, words].rearrange("p (h u n) -> p h n u", n=HALF, u=2),
             )
 
-        def quantize_half(name, g, h):
-            quantize(name, g, slice(HALF * h, HALF * (h + 1)), tiles[name + "_in", g, h])
-
-        def finish(name, g):
-            join_pairs(name, g, 0)
-            join_pairs(name, g, 1)
-            quantize_half(name, g, 0)
-            quantize_half(name, g, 1)
+        def quantize_joined(name, g, halves):
+            first, last = HALF * halves[0], HALF * (halves[-1] + 1)
+            quantize(name, g, slice(first, last), tiles[name + "_in", g][:, 4 * first : 4 * last])
 
         def drain_group(g):
             for c in range(COV_PASSES):
                 for b in range(2):
-                    drain_cov(g, c, b)
+                    drain_cov(g, c, b, nc.scalar.copy)
 
-        def score_group(g):
-            for h in range(2):
-                score(g, [h])
-                member(g, h, 0)
-                member(g, h, 1)
+        def score_group(g, quarters):
+            for q in quarters:
+                score(g, q)
+                member(g, q)
 
         def load_v_scales(g):
             load_scale_rows(v_scale_raw[g], v_scales, slice(512 * g, 512 * (g + 1)), range(4))
@@ -269,6 +278,7 @@ def tile_local_moran_typology_s12_kernel(tc, v_words, v_scales, y_words, y_scale
                 )
             result = kept(("out", m, cols.start), [P, width], F32)
             scale_out(result[:], sums[:, 0:width])
+            release(("assoc", m, cols.start))
             nc.sync.dma_start(out=out[P * m : P * (m + 1), cols], in_=result[:])
 
         def scale_on_scalar(result, sums):
@@ -292,20 +302,24 @@ def tile_local_moran_typology_s12_kernel(tc, v_words, v_scales, y_words, y_scale
 
         pieces = [[0], [1], [2, 3]]
         whole = [0, 1, 2, 3]
-        load_v_scales(0)
-        load_scale_rows(y_scale_words, y_scales, slice(0, 512), range(2))
+        both = [0, 1]
+        on_vector = nc.vector.tensor_copy
+        on_scalar = nc.scalar.copy
+        left, right = slice(0, HALF), slice(HALF, R)
         load_v(0, pieces[0])
         load_y(pieces[0])
-        load_scale_rows(y_scale_words, y_scales, slice(0, 512), range(2, 4))
+        load_v_scales(0)
+        load_scale_rows(y_scale_words, y_scales, slice(0, 512), range(4))
         for piece in pieces[1:]:
             load_v(0, piece)
             load_y(piece)
-        load_v_scales(1)
-        load_v(1, whole)
-        load_loadings(0)
-        load_x(0)
         load_cov(0, 0)
         load_cov(0, 1)
+        load_v_scales(1)
+        load_v(1, whole)
+        load_x(0)
+        load_loadings(0)
+        load_loadings(1)
         load_x(1)
 
         sort_v_scales(0)
@@ -314,96 +328,101 @@ def tile_local_moran_typology_s12_kernel(tc, v_words, v_scales, y_words, y_scale
         load_v_scales(2)
         load_v(2, whole)
         load_cov(1, 0)
-        load_loadings(1)
         load_cov(1, 1)
         load_x(2)
-        lag(0, [0, 1])
-        sort_v_scales(1)
-        sort_v(1, whole)
-        interleave_loadings(0, slice(0, R), nc.vector.tensor_copy)
-        lag(1, [0])
-        lag(1, [1])
-        local(0, 0, 0)
-        quantize_loadings(0)
-        local(0, 0, 1)
-        local(0, 1, 0)
-        local(0, 1, 1)
-        sort_cov(0, 0, nc.scalar.copy)
-        sort_cov(0, 1, nc.scalar.copy)
+        lag(0, both)
+        sort_cov(0, 0, on_vector)
+        sort_cov(0, 1, on_vector)
         load_cov(2, 0)
         load_cov(2, 1)
         load_v_scales(3)
         load_v(3, whole)
-        join_pairs("local", 0, 0)
-        local(1, 0, 0)
-        quantize_half("local", 0, 0)
-        local(1, 0, 1)
+        sort_v_scales(1)
+        sort_v(1, whole)
+
+        transpose_cov(0)
+        drain_group(0)
+        lag_half(1, 0)
+        quantize_cov(0, 0)
+        local(0, 0, 0)
+        local(0, 0, 1)
+        lag_half(1, 1)
+        quantize_cov(0, 1)
+        interleave_loadings(0, left, on_scalar)
+        interleave_loadings(0, right, on_scalar)
+        interleave_loadings(1, left, on_vector)
+        quantize_loadings(0, left)
+        interleave_loadings(1, right, on_scalar)
+        quantize_loadings(1, left)
+        local(0, 1, 0)
+        quantize_loadings(0, right)
+        quantize_loadings(1, right)
         sort_v_scales(2)
+        local(0, 1, 1)
+        score_group(0, [0, 1])
+        sort_cov(1, 0, on_scalar)
+        score_group(0, [2, 3])
         sort_v(2, whole)
+        lag_half(2, 0)
+        local(1, 0, 0)
+        local(1, 0, 1)
+        sort_cov(1, 1, on_vector)
         local(1, 1, 0)
         local(1, 1, 1)
-        transpose_cov(0)
-        lag(2, [0])
-        drain_group(0)
-        sort_cov(1, 0, nc.vector.tensor_copy)
-        quantize_cov(0, 0)
-        interleave_loadings(1, slice(0, HALF), nc.vector.tensor_copy)
-        interleave_loadings(1, slice(HALF, R), nc.scalar.copy)
-        sort_cov(1, 1, nc.vector.tensor_copy)
-        quantize_cov(0, 1)
         load_cov(3, 0)
         load_cov(3, 1)
         load_x(3)
-        quantize_loadings(1)
-        local(2, 0, 0)
-        local(2, 0, 1)
 
         transpose_cov(1)
         drain_group(1)
-        score_group(0)
-        lag(2, [1])
-        join_pairs("local", 0, 1)
+        lag_half(2, 1)
+        local(2, 0, 0)
+        local(2, 0, 1)
+        join_pairs("local", 0, both)
         quantize_cov(1, 0)
-        sort_cov(2, 0, nc.vector.tensor_copy)
         quantize_cov(1, 1)
-        sort_cov(2, 1, nc.vector.tensor_copy)
-        quantize_half("local", 0, 1)
+        quantize_joined("local", 0, both)
+        sort_cov(2, 0, on_scalar)
+        sort_cov(2, 1, on_scalar)
         local(2, 1, 0)
         local(2, 1, 1)
+        score_group(1, whole)
+        sort_v_scales(3)
+        sort_v(3, whole)
+        join_pairs("local", 1, both)
+        quantize_joined("member", 0, both)
 
         transpose_cov(2)
         drain_group(2)
-        score_group(1)
-        sort_v_scales(3)
-        sort_v(3, whole)
-        lag(3, [0])
-        finish("member", 0)
+        lag_half(3, 0)
+        sort_cov(3, 0, on_vector)
+        sort_cov(3, 1, on_vector)
         quantize_cov(2, 0)
-        sort_cov(3, 0, nc.vector.tensor_copy)
+        quantize_joined("local", 1, both)
         quantize_cov(2, 1)
-        sort_cov(3, 1, nc.vector.tensor_copy)
-        finish("local", 1)
         local(3, 0, 0)
         local(3, 0, 1)
 
         transpose_cov(3)
         drain_group(3)
-        score_group(2)
-        finish("member", 1)
+        score_group(2, whole)
         quantize_cov(3, 0)
-        join_pairs("local", 3, 0)
+        quantize_joined("member", 1, both)
         quantize_cov(3, 1)
-        quantize_half("local", 3, 0)
-        finish("local", 2)
+        join_pairs("local", 2, both)
+        join_pairs("local", 3, [0])
+        quantize_joined("local", 2, both)
 
-        score_group(3)
-        lag(3, [1])
-        finish("member", 2)
-        finish("member", 3)
+        score_group(3, whole)
+        lag_half(3, 1)
+        quantize_joined("local", 3, [0])
+        quantize_joined("member", 2, both)
+        quantize_joined("member", 3, [0])
         local(3, 1, 0)
+        quantize_joined("member", 3, [1])
         local(3, 1, 1)
-        join_pairs("local", 3, 1)
-        quantize_half("local", 3, 1)
+        join_pairs("local", 3, [1])
+        quantize_joined("local", 3, [1])
         for m in range(3):
             assoc(m, slice(0, R), scale_on_scalar)
         assoc(3, slice(0, HALF), scale_on_scalar)

@@ -196,20 +196,18 @@ def tile_local_moran_typology_s12_kernel(tc, v_words, v_scales, y_words, y_scale
                 for c in range(LAG_PASSES):
                     lag_pass(g, h, u, 1, c)
 
-        def score(g, q):
-            sums = bank(("score", g, q))
-            for t in range(4):
-                for c in range(COV_PASSES):
-                    index = COV_PASSES * g + c
-                    nc.tensor.matmul_mx(
-                        out=sums[:, P * t : P * (t + 1)],
-                        lhsT=tiles["cov", index][:, P * t : P * (t + 1)].bitcast(FP8X4),
-                        lhsT_scale=tiles["cov_scale", index][:, P * t : P * (t + 1)],
-                        rhs=tiles["load", c][:, P * q : P * (q + 1)].bitcast(FP8X4),
-                        rhs_scale=tiles["load_scale", c][:, P * q : P * (q + 1)],
-                        start=(c == 0),
-                        stop=(c == COV_PASSES - 1),
-                    )
+        def score_pass(g, h, u, e, c):
+            t = 2 * u + e
+            index = COV_PASSES * g + c
+            nc.tensor.matmul_mx(
+                out=tiles["score", g, h, u][:, HALF * e : HALF * (e + 1)],
+                lhsT=tiles["cov", index][:, P * t : P * (t + 1)].bitcast(FP8X4),
+                lhsT_scale=tiles["cov_scale", index][:, P * t : P * (t + 1)],
+                rhs=tiles["load", c][:, HALF * h : HALF * (h + 1)].bitcast(FP8X4),
+                rhs_scale=tiles["load_scale", c][:, HALF * h : HALF * (h + 1)],
+                start=(c == 0),
+                stop=(c == COV_PASSES - 1),
+            )
 
         def pair_view(name, g, h, u):
             if (name + "_pairs", g) not in tiles:
@@ -227,21 +225,19 @@ def tile_local_moran_typology_s12_kernel(tc, v_words, v_scales, y_words, y_scale
             )
             release(("lag", g, h, u))
 
-        def member(g, q):
-            if q == 0:
-                passing(("member_in", g), [P, 4 * 512], BF16, 2)
+        def member(g, h, u):
             nc.scalar.activation(
-                out=tiles["member_in", g][:, 4 * P * q : 4 * P * (q + 1)].rearrange("p (n t) -> p n t", t=4),
-                in_=tiles["score", g, q][:].rearrange("p (t n) -> p n t", t=4),
+                out=pair_view("member", g, h, u),
+                in_=tiles["score", g, h, u][:].rearrange("p (e n i) -> p n e i", e=2, i=4),
                 func=ACT.Relu,
             )
-            release(("score", g, q))
+            release(("score", g, h, u))
 
-        def join_pairs(name, g, halves):
+        def join_pairs(name, g, halves, copy):
             if (name + "_in", g) not in tiles:
                 passing((name + "_in", g), [P, 4 * 512], BF16, 2)
             words = slice(2 * HALF * halves[0], 2 * HALF * (halves[-1] + 1))
-            nc.vector.tensor_copy(
+            copy(
                 out=tiles[name + "_in", g][:].bitcast(F32)[:, words].rearrange("p (h n u) -> p h n u", n=HALF, u=2),
                 in_=tiles[name + "_pairs", g][:].bitcast(F32)[:, words].rearrange("p (h u n) -> p h n u", n=HALF, u=2),
             )
@@ -255,20 +251,26 @@ def tile_local_moran_typology_s12_kernel(tc, v_words, v_scales, y_words, y_scale
                 for b in range(2):
                     drain_cov(g, c, b, nc.scalar.copy)
 
-        def score_group(g, quarters):
-            for q in quarters:
-                score(g, q)
-                member(g, q)
+        def score_group(g, halves):
+            banks = [(h, u) for h in halves for u in range(2)]
+            for h, u in banks:
+                bank(("score", g, h, u))
+                score_pass(g, h, u, 0, 0)
+            for h, u in banks:
+                score_pass(g, h, u, 0, 1)
+                score_pass(g, h, u, 1, 0)
+                score_pass(g, h, u, 1, 1)
+                member(g, h, u)
 
         def load_v_scales(g):
             load_scale_rows(v_scale_raw[g], v_scales, slice(512 * g, 512 * (g + 1)), range(4))
 
-        def assoc(m, cols, scale_out):
-            width = cols.stop - cols.start
-            sums = bank(("assoc", m, cols.start))
-            for g in range(GROUPS):
+        def assoc(m, cols, groups):
+            if groups[0] == 0:
+                bank(("assoc", m, cols.start))
+            for g in groups:
                 nc.tensor.matmul_mx(
-                    out=sums[:, 0:width],
+                    out=tiles["assoc", m, cols.start][:, 0 : cols.stop - cols.start],
                     lhsT=tiles["local", g][:, P * m : P * (m + 1)].bitcast(FP8X4),
                     lhsT_scale=tiles["local_scale", g][:, P * m : P * (m + 1)],
                     rhs=tiles["member", g][:, cols].bitcast(FP8X4),
@@ -276,8 +278,11 @@ def tile_local_moran_typology_s12_kernel(tc, v_words, v_scales, y_words, y_scale
                     start=(g == 0),
                     stop=(g == GROUPS - 1),
                 )
+
+        def store(m, cols, scale_out):
+            width = cols.stop - cols.start
             result = kept(("out", m, cols.start), [P, width], F32)
-            scale_out(result[:], sums[:, 0:width])
+            scale_out(result[:], tiles["assoc", m, cols.start][:, 0:width])
             release(("assoc", m, cols.start))
             nc.sync.dma_start(out=out[P * m : P * (m + 1), cols], in_=result[:])
 
@@ -320,13 +325,13 @@ def tile_local_moran_typology_s12_kernel(tc, v_words, v_scales, y_words, y_scale
         load_x(0)
         load_loadings(0)
         load_loadings(1)
-        load_x(1)
+        load_v_scales(2)
 
         sort_v_scales(0)
         for piece in pieces:
             sort_v(0, piece)
-        load_v_scales(2)
         load_v(2, whole)
+        load_x(1)
         load_cov(1, 0)
         load_cov(1, 1)
         load_x(2)
@@ -356,16 +361,17 @@ def tile_local_moran_typology_s12_kernel(tc, v_words, v_scales, y_words, y_scale
         quantize_loadings(1, left)
         local(0, 1, 0)
         quantize_loadings(0, right)
+        local(0, 1, 1)
         quantize_loadings(1, right)
         sort_v_scales(2)
-        local(0, 1, 1)
-        score_group(0, [0, 1])
+        score_group(0, [0])
         sort_cov(1, 0, on_scalar)
-        score_group(0, [2, 3])
+        score_group(0, [1])
         sort_v(2, whole)
         lag_half(2, 0)
         local(1, 0, 0)
         local(1, 0, 1)
+        join_pairs("local", 0, both, on_vector)
         sort_cov(1, 1, on_vector)
         local(1, 1, 0)
         local(1, 1, 1)
@@ -378,18 +384,18 @@ def tile_local_moran_typology_s12_kernel(tc, v_words, v_scales, y_words, y_scale
         lag_half(2, 1)
         local(2, 0, 0)
         local(2, 0, 1)
-        join_pairs("local", 0, both)
+        quantize_joined("local", 0, both)
         quantize_cov(1, 0)
         quantize_cov(1, 1)
-        quantize_joined("local", 0, both)
+        join_pairs("member", 0, both, on_vector)
         sort_cov(2, 0, on_scalar)
         sort_cov(2, 1, on_scalar)
         local(2, 1, 0)
         local(2, 1, 1)
-        score_group(1, whole)
+        score_group(1, both)
         sort_v_scales(3)
         sort_v(3, whole)
-        join_pairs("local", 1, both)
+        join_pairs("local", 1, both, on_vector)
         quantize_joined("member", 0, both)
 
         transpose_cov(2)
@@ -405,25 +411,37 @@ def tile_local_moran_typology_s12_kernel(tc, v_words, v_scales, y_words, y_scale
 
         transpose_cov(3)
         drain_group(3)
-        score_group(2, whole)
+        score_group(2, [0])
+        score_group(2, [1])
+        join_pairs("member", 1, both, on_vector)
         quantize_cov(3, 0)
-        quantize_joined("member", 1, both)
         quantize_cov(3, 1)
-        join_pairs("local", 2, both)
-        join_pairs("local", 3, [0])
+        join_pairs("local", 3, [0], on_vector)
+        join_pairs("local", 2, both, on_vector)
+        quantize_joined("member", 1, both)
         quantize_joined("local", 2, both)
 
-        score_group(3, whole)
+        score_group(3, both)
         lag_half(3, 1)
+        join_pairs("member", 2, both, on_vector)
         quantize_joined("local", 3, [0])
         quantize_joined("member", 2, both)
-        quantize_joined("member", 3, [0])
+        join_pairs("member", 3, [0], on_vector)
+        join_pairs("member", 3, [1], on_scalar)
         local(3, 1, 0)
+        quantize_joined("member", 3, [0])
         quantize_joined("member", 3, [1])
         local(3, 1, 1)
-        join_pairs("local", 3, [1])
+        join_pairs("local", 3, [1], on_vector)
         quantize_joined("local", 3, [1])
-        for m in range(3):
-            assoc(m, slice(0, R), scale_on_scalar)
-        assoc(3, slice(0, HALF), scale_on_scalar)
-        assoc(3, slice(HALF, R), scale_on_vector)
+        every = slice(0, R)
+        assoc(0, every, [0, 1, 2])
+        assoc(1, every, [0, 1, 2])
+        for m in range(2):
+            assoc(m, every, [3])
+            store(m, every, scale_on_scalar)
+        for m in range(2, 4):
+            assoc(m, left, whole)
+            store(m, left, scale_on_scalar)
+            assoc(m, right, whole)
+            store(m, right, scale_on_vector)

import math
from contextlib import ExitStack

import concourse.mybir as mybir
from concourse.masks import make_identity

S, PAIRS, C, R = 2048, 512, 1024, 512
FLOPS = 2 * S * S * PAIRS + 2 * S * C * R + 2 * S * PAIRS * R

F32 = mybir.dt.float32
BF16 = mybir.dt.bfloat16
I32 = mybir.dt.int32
U32 = mybir.dt.uint32
U8 = mybir.dt.uint8
FP8X4 = mybir.dt.float8_e4m3fn_x4
FP4X4 = mybir.dt.float4_e2m1fn_x4
ACT = mybir.ActivationFunctionType
ALU = mybir.AluOpType

P = 128
K_PASS = 512
GROUPS = S // K_PASS
LAG_PASSES = S // K_PASS
COV_PASSES = C // K_PASS
HALF = 256
BANKS = 8


def tile_local_moran_typology_s12_kernel(tc, v_words, v_scales, y_words, y_scales, x, cov, load, out):
    nc = tc.nc
    with ExitStack() as ctx:
        keep = ctx.enter_context(tc.tile_pool(name="keep", bufs=1))
        work = ctx.enter_context(tc.tile_pool(name="work", bufs=2))
        psum = ctx.enter_context(tc.psum_pool(name="psum", bufs=1))
        ctx.enter_context(tc.manual_schedule())

        tiles = {}
        ring = list(range(BANKS))
        held = {}

        def kept(key, shape, dtype):
            name = "t_" + "_".join(str(part) for part in key)
            tiles[key] = keep.tile(shape, dtype, name=name, align_bytes=64)
            return tiles[key]

        def passing(key, shape, dtype, bufs):
            name = "t_" + "_".join(str(part) for part in key)
            tiles[key] = work.tile(shape, dtype, name=name, tag=key[0], bufs=bufs, align_bytes=64)
            return tiles[key]

        def bank(key):
            number = ring.pop(0)
            held[key] = number
            name = "b_" + "_".join(str(part) for part in key)
            tiles[key] = psum.tile([P, 512], F32, name=name, tag="bank%d" % number)
            return tiles[key]

        def release(key):
            ring.append(held[key])

        def load_scale_rows(plane, scales, cols, rows):
            by_row = scales.rearrange("g (q r) n -> r q g n", r=4)
            for r in rows:
                nc.sync.dma_start(out=plane[r:P:32, :, :], in_=by_row[r][:, :, cols].bitcast(I32))

        def load_v(g, passes):
            raw = passing(("v_raw", g, passes[0]), [P, len(passes), 256], I32, 4)
            words = v_words[passes[0] : passes[-1] + 1, :, 1024 * g : 1024 * (g + 1)]
            nc.sync.dma_start(out=raw[:], in_=words.rearrange("c p n -> p c n").bitcast(I32))

        def load_y(passes):
            codes = kept(("y", passes[0]), [P, len(passes) * 1024], U8)
            words = y_words[passes[0] : passes[-1] + 1, :, :]
            nc.sync.dma_start(
                out=codes[:].bitcast(I32).rearrange("p (c n) -> p c n", c=len(passes)),
                in_=words.rearrange("c p n -> p c n").bitcast(I32),
            )
            for i, c in enumerate(passes):
                tiles["y_pass", c] = codes[:, 1024 * i : 1024 * (i + 1)]

        def load_x(g):
            rows = passing(("x", g), [P, 4, PAIRS], BF16, 4)
            by_lane = x[K_PASS * g : K_PASS * (g + 1), :].rearrange("(a t l) n -> l a t n", t=4, l=4)
            for lane in range(4):
                nc.sync.dma_start(out=rows[lane:P:4, :, :], in_=by_lane[lane])

        def load_cov(g, b):
            raw = passing(("cov_raw", g, b), [P, 2 * C], BF16, 4)
            first = K_PASS * g + 256 * b
            nc.sync.dma_start(
                out=raw[:].rearrange("p (a k) -> p a k", a=2),
                in_=cov[first : first + 256, :].rearrange("(a p) k -> p a k", p=P),
            )

        def load_loadings(c):
            raw = kept(("load_raw", c), [P, 4, R], BF16)
            nc.sync.dma_start(out=raw[:], in_=load[K_PASS * c : K_PASS * (c + 1), :].rearrange("(p j) n -> p j n", j=4))

        def sort_v(g, passes):
            n = len(passes)
            codes = passing(("v", g, passes[0]), [P, n * 1024], U8, 4)
            nc.vector.tensor_copy(
                out=codes[:].bitcast(I32).rearrange("p (c t a l) -> p c t a l", c=n, t=4, l=2),
                in_=tiles["v_raw", g, passes[0]][:].rearrange("p c (a t l) -> p c t a l", t=4, l=2),
            )
            for i, c in enumerate(passes):
                tiles["v_pass", g, c] = codes[:, 1024 * i : 1024 * (i + 1)]

        def sort_v_scales(g):
            plane = passing(("v_scale", g), [P, LAG_PASSES * 512], U8, 2)
            nc.vector.tensor_copy(
                out=plane[:].bitcast(I32).rearrange("p (c t a b) -> p c a t b", c=LAG_PASSES, t=4, b=4),
                in_=v_scale_raw[g][:].rearrange("p c (a b t) -> p c a t b", b=4, t=4),
            )

        def interleave_loadings(c, cols, copy):
            if ("load_in", c) not in tiles:
                kept(("load_in", c), [P, 4 * R], BF16)
            grouped = tiles["load_in", c][:, 4 * cols.start : 4 * cols.stop]
            copy(
                out=grouped.rearrange("p (n i j) -> p n j i", i=4, j=4),
                in_=tiles["load_raw", c][:, :, cols].rearrange("p j (n i) -> p n j i", i=4),
            )

        def quantize(name, index, cols, source):
            if (name, index) not in tiles:
                kept((name, index), [P, 512], U32)
                kept((name + "_scale", index), [P, 512], U8)
            nc.vector.quantize_mx(
                out=tiles[name, index][:, cols].bitcast(FP8X4),
                scales=tiles[name + "_scale", index][:, cols],
                in_=source,
            )

        def quantize_loadings(c, cols):
            quantize("load", c, cols, tiles["load_in", c][:, 4 * cols.start : 4 * cols.stop])

        def sort_cov(g, b, copy):
            words = passing(("cov_words", g, b), [P, C], F32, 4)
            copy(
                out=words[:].rearrange("p (j u k) -> p j u k", u=2, k=P),
                in_=tiles["cov_raw", g, b][:].bitcast(F32).rearrange("p (j k u) -> p j u k", u=2, k=P),
            )

        def transpose_cov(g):
            for c in range(COV_PASSES):
                for b in range(2):
                    turned = bank(("cov_t", g, c, b))
                    words = tiles["cov_words", g, b]
                    for u in range(2):
                        for a in range(2):
                            src = (2 * (COV_PASSES * a + c) + u) * P
                            dst = (2 * u + a) * P
                            nc.tensor.transpose(turned[:, dst : dst + P], words[:, src : src + P], identity[:])

        def drain_cov(g, c, b, copy):
            if b == 0:
                passing(("cov_in", g, c), [P, 2048], BF16, 3)
            dst = tiles["cov_in", g, c][:].bitcast(F32).rearrange("p (t w) -> p t w", t=4)[:, :, P * b : P * (b + 1)]
            copy(
                out=dst.rearrange("p t (a l u) -> p t a l u", l=4, u=2),
                in_=tiles["cov_t", g, c, b][:].rearrange("p (u a t l) -> p t a l u", u=2, t=4, l=4),
            )
            release(("cov_t", g, c, b))

        def quantize_cov(g, c):
            quantize("cov", COV_PASSES * g + c, slice(0, 512), tiles["cov_in", g, c][:])

        def lag_pass(g, h, u, e, c):
            t = 2 * u + e
            nc.tensor.matmul_mx(
                out=tiles["lag", g, h, u][:, HALF * e : HALF * (e + 1)],
                lhsT=tiles["v_pass", g, c][:, 256 * t : 256 * (t + 1)].bitcast(FP4X4),
                lhsT_scale=tiles["v_scale", g][:, 512 * c + P * t : 512 * c + P * (t + 1)],
                rhs=tiles["y_pass", c][:, 2 * HALF * h : 2 * HALF * (h + 1)].bitcast(FP4X4),
                rhs_scale=y_scale[:, 512 * c + HALF * h : 512 * c + HALF * (h + 1)],
                start=(c == 0),
                stop=(c == LAG_PASSES - 1),
            )

        def lag_half(g, h):
            for u in range(2):
                bank(("lag", g, h, u))
                for e in range(2):
                    for c in range(LAG_PASSES):
                        lag_pass(g, h, u, e, c)

        def lag(g, halves):
            banks = [(h, u) for h in halves for u in range(2)]
            for h, u in banks:
                bank(("lag", g, h, u))
            for c in range(LAG_PASSES):
                for h, u in banks:
                    lag_pass(g, h, u, 0, c)
            for h, u in banks:
                for c in range(LAG_PASSES):
                    lag_pass(g, h, u, 1, c)

        def score_pass(g, h, u, e, c):
            t = 2 * u + e
            index = COV_PASSES * g + c
            nc.tensor.matmul_mx(
                out=tiles["score", g, h, u][:, HALF * e : HALF * (e + 1)],
                lhsT=tiles["cov", index][:, P * t : P * (t + 1)].bitcast(FP8X4),
                lhsT_scale=tiles["cov_scale", index][:, P * t : P * (t + 1)],
                rhs=tiles["load", c][:, HALF * h : HALF * (h + 1)].bitcast(FP8X4),
                rhs_scale=tiles["load_scale", c][:, HALF * h : HALF * (h + 1)],
                start=(c == 0),
                stop=(c == COV_PASSES - 1),
            )

        def pair_view(name, g, h, u):
            if (name + "_pairs", g) not in tiles:
                passing((name + "_pairs", g), [P, 4 * 512], BF16, 3)
            first = 2 * HALF * (2 * h + u)
            pairs = tiles[name + "_pairs", g][:, first : first + 2 * HALF]
            return pairs.rearrange("p (n i e) -> p n e i", i=4, e=2)

        def local(g, h, u):
            nc.vector.tensor_tensor(
                out=pair_view("local", g, h, u),
                in0=tiles["lag", g, h, u][:].rearrange("p (e n i) -> p n e i", e=2, i=4),
                in1=tiles["x", g][:, 2 * u : 2 * u + 2, HALF * h : HALF * (h + 1)].rearrange("p e (n i) -> p n e i", i=4),
                op=ALU.mult,
            )
            release(("lag", g, h, u))

        def member(g, h, u):
            nc.scalar.activation(
                out=pair_view("member", g, h, u),
                in_=tiles["score", g, h, u][:].rearrange("p (e n i) -> p n e i", e=2, i=4),
                func=ACT.Relu,
            )
            release(("score", g, h, u))

        def join_pairs(name, g, halves, copy):
            if (name + "_in", g) not in tiles:
                passing((name + "_in", g), [P, 4 * 512], BF16, 2)
            words = slice(2 * HALF * halves[0], 2 * HALF * (halves[-1] + 1))
            copy(
                out=tiles[name + "_in", g][:].bitcast(F32)[:, words].rearrange("p (h n u) -> p h n u", n=HALF, u=2),
                in_=tiles[name + "_pairs", g][:].bitcast(F32)[:, words].rearrange("p (h u n) -> p h n u", n=HALF, u=2),
            )

        def quantize_joined(name, g, halves):
            first, last = HALF * halves[0], HALF * (halves[-1] + 1)
            quantize(name, g, slice(first, last), tiles[name + "_in", g][:, 4 * first : 4 * last])

        def drain_group(g):
            for c in range(COV_PASSES):
                for b in range(2):
                    drain_cov(g, c, b, nc.scalar.copy)

        def score_group(g, halves):
            banks = [(h, u) for h in halves for u in range(2)]
            for h, u in banks:
                bank(("score", g, h, u))
                score_pass(g, h, u, 0, 0)
            for h, u in banks:
                score_pass(g, h, u, 0, 1)
                score_pass(g, h, u, 1, 0)
                score_pass(g, h, u, 1, 1)
                member(g, h, u)

        def load_v_scales(g):
            load_scale_rows(v_scale_raw[g], v_scales, slice(512 * g, 512 * (g + 1)), range(4))

        def assoc(m, cols, groups):
            if groups[0] == 0:
                bank(("assoc", m, cols.start))
            for g in groups:
                nc.tensor.matmul_mx(
                    out=tiles["assoc", m, cols.start][:, 0 : cols.stop - cols.start],
                    lhsT=tiles["local", g][:, P * m : P * (m + 1)].bitcast(FP8X4),
                    lhsT_scale=tiles["local_scale", g][:, P * m : P * (m + 1)],
                    rhs=tiles["member", g][:, cols].bitcast(FP8X4),
                    rhs_scale=tiles["member_scale", g][:, cols],
                    start=(g == 0),
                    stop=(g == GROUPS - 1),
                )

        def store(m, cols, scale_out):
            width = cols.stop - cols.start
            result = kept(("out", m, cols.start), [P, width], F32)
            scale_out(result[:], tiles["assoc", m, cols.start][:, 0:width])
            release(("assoc", m, cols.start))
            nc.sync.dma_start(out=out[P * m : P * (m + 1), cols], in_=result[:])

        def scale_on_scalar(result, sums):
            nc.scalar.activation(out=result, in_=sums, func=ACT.Copy, scale=1.0 / math.sqrt(S))

        def scale_on_vector(result, sums):
            nc.vector.tensor_scalar_mul(out=result, in0=sums, scalar1=1.0 / math.sqrt(S))

        v_scale_raw = [kept(("v_scale_raw", g), [P, LAG_PASSES, P], I32) for g in range(GROUPS)]
        y_scale = kept(("y_scale",), [P, LAG_PASSES * 512], U8)
        y_scale_words = y_scale[:].bitcast(I32).rearrange("p (c n) -> p c n", c=LAG_PASSES)
        identity = kept(("identity",), [P, P], F32)
        warm = kept(("warm",), [P, 2], F32)
        nc.vector.memset(v_scale_raw[0][:], 0)
        nc.vector.memset(y_scale_words, 0)
        for g in range(1, GROUPS):
            nc.vector.memset(v_scale_raw[g][:], 0)
        nc.vector.memset(identity[:], 0.0)
        make_identity(nc, identity[:], nomemset=True)
        nc.scalar.activation(out=warm[:, 0:1], in_=identity[:, 0:1], func=ACT.Relu)

        pieces = [[0], [1], [2, 3]]
        whole = [0, 1, 2, 3]
        both = [0, 1]
        on_vector = nc.vector.tensor_copy
        on_scalar = nc.scalar.copy
        left, right = slice(0, HALF), slice(HALF, R)
        load_v(0, pieces[0])
        load_y(pieces[0])
        load_v_scales(0)
        load_scale_rows(y_scale_words, y_scales, slice(0, 512), range(4))
        for piece in pieces[1:]:
            load_v(0, piece)
            load_y(piece)
        load_cov(0, 0)
        load_cov(0, 1)
        load_v_scales(1)
        load_v(1, whole)
        load_x(0)
        load_loadings(0)
        load_loadings(1)
        load_v_scales(2)

        sort_v_scales(0)
        for piece in pieces:
            sort_v(0, piece)
        load_v(2, whole)
        load_x(1)
        load_cov(1, 0)
        load_cov(1, 1)
        load_x(2)
        lag(0, both)
        sort_cov(0, 0, on_vector)
        sort_cov(0, 1, on_vector)
        load_cov(2, 0)
        load_cov(2, 1)
        load_v_scales(3)
        load_v(3, whole)
        sort_v_scales(1)
        sort_v(1, whole)

        transpose_cov(0)
        drain_group(0)
        lag_half(1, 0)
        quantize_cov(0, 0)
        local(0, 0, 0)
        local(0, 0, 1)
        lag_half(1, 1)
        quantize_cov(0, 1)
        interleave_loadings(0, left, on_scalar)
        interleave_loadings(0, right, on_scalar)
        interleave_loadings(1, left, on_vector)
        quantize_loadings(0, left)
        interleave_loadings(1, right, on_scalar)
        quantize_loadings(1, left)
        local(0, 1, 0)
        quantize_loadings(0, right)
        local(0, 1, 1)
        quantize_loadings(1, right)
        sort_v_scales(2)
        score_group(0, [0])
        sort_cov(1, 0, on_scalar)
        score_group(0, [1])
        sort_v(2, whole)
        lag_half(2, 0)
        local(1, 0, 0)
        local(1, 0, 1)
        join_pairs("local", 0, both, on_vector)
        sort_cov(1, 1, on_vector)
        local(1, 1, 0)
        local(1, 1, 1)
        load_cov(3, 0)
        load_cov(3, 1)
        load_x(3)

        transpose_cov(1)
        drain_group(1)
        lag_half(2, 1)
        local(2, 0, 0)
        local(2, 0, 1)
        quantize_joined("local", 0, both)
        quantize_cov(1, 0)
        quantize_cov(1, 1)
        join_pairs("member", 0, both, on_vector)
        sort_cov(2, 0, on_scalar)
        sort_cov(2, 1, on_scalar)
        local(2, 1, 0)
        local(2, 1, 1)
        score_group(1, both)
        sort_v_scales(3)
        sort_v(3, whole)
        join_pairs("local", 1, both, on_vector)
        quantize_joined("member", 0, both)

        transpose_cov(2)
        drain_group(2)
        lag_half(3, 0)
        sort_cov(3, 0, on_vector)
        sort_cov(3, 1, on_vector)
        quantize_cov(2, 0)
        quantize_joined("local", 1, both)
        quantize_cov(2, 1)
        local(3, 0, 0)
        local(3, 0, 1)

        transpose_cov(3)
        drain_group(3)
        score_group(2, [0])
        score_group(2, [1])
        join_pairs("member", 1, both, on_vector)
        quantize_cov(3, 0)
        quantize_cov(3, 1)
        join_pairs("local", 3, [0], on_vector)
        join_pairs("local", 2, both, on_vector)
        quantize_joined("member", 1, both)
        quantize_joined("local", 2, both)

        score_group(3, both)
        lag_half(3, 1)
        join_pairs("member", 2, both, on_vector)
        quantize_joined("local", 3, [0])
        quantize_joined("member", 2, both)
        join_pairs("member", 3, [0], on_vector)
        join_pairs("member", 3, [1], on_scalar)
        local(3, 1, 0)
        quantize_joined("member", 3, [0])
        quantize_joined("member", 3, [1])
        local(3, 1, 1)
        join_pairs("local", 3, [1], on_vector)
        quantize_joined("local", 3, [1])
        every = slice(0, R)
        assoc(0, every, [0, 1, 2])
        assoc(1, every, [0, 1, 2])
        for m in range(2):
            assoc(m, every, [3])
            store(m, every, scale_on_scalar)
        for m in range(2, 4):
            assoc(m, left, whole)
            store(m, left, scale_on_scalar)
            assoc(m, right, whole)
            store(m, right, scale_on_vector)
